import numpy as np
import ml_dtypes


def mxq(x, axis, fmt="e4m3"):
    dtype, down = {"e4m3": (ml_dtypes.float8_e4m3fn, 7), "e5m2": (ml_dtypes.float8_e5m2, 14)}[fmt]
    v = np.moveaxis(np.asarray(x, np.float32).astype(ml_dtypes.bfloat16).astype(np.float64), axis, -1)
    blocks = v.reshape(v.shape[:-1] + (-1, 32))
    amax = np.abs(blocks).max(-1, keepdims=True)
    byte = np.maximum(np.where(amax > 0, np.frexp(amax)[1] - 1 + 127, 0) - down, 1)
    scale = np.exp2(byte - 127.0)
    codes = (blocks / scale).astype(np.float32).astype(dtype).astype(np.float64)
    return np.moveaxis((codes * scale).reshape(v.shape), -1, axis)


WIDE = False


def mx_kscale(k):
    if not WIDE:
        return np.ones(k)
    levels = np.array([10, -10, 5, -5, 0])
    if k % 512:
        return np.exp2(np.random.permutation(np.resize(levels, k // 32))).repeat(32)
    a = np.empty((k // 512, 16))
    for p in range(k // 512):
        a[p, :8] = np.random.permutation(np.resize(levels, 8))
        for g in range(8):
            far = levels[np.abs(levels - a[p, g]) >= 10]
            a[p, g + 8] = far[np.random.randint(len(far))]
    return np.exp2(a.ravel()).repeat(32)


BF16 = ml_dtypes.bfloat16


def bf(x):
    return np.asarray(x, np.float32).astype(BF16)


def f64(x):
    return np.asarray(x).astype(np.float64)


E2M1 = np.array([0.0, 0.5, 1.0, 1.5, 2.0, 3.0, 4.0, 6.0, -0.0, -0.5, -1.0, -1.5, -2.0, -3.0, -4.0, -6.0])


def pack_weight(w, fmt):
    k, n = w.shape
    w = f64(bf(w)).reshape(k // 32, 32, n)
    amax = np.abs(w).max(1)
    if fmt == "e4m3":
        byte = np.frexp(amax)[1] - 1 + 127 - 7
    else:
        mant, ex = np.frexp(amax / 6.0)
        byte = np.where(mant > 0.5, ex, ex - 1) + 127
    byte = np.clip(np.where(amax > 0, byte, 1), 1, 254)
    scaled = (w * np.exp2(127.0 - byte)[:, None, :]).reshape(k, n).astype(np.float32)
    by_word = np.ascontiguousarray(scaled.reshape(k // 512, 128, 4, n).transpose(0, 1, 3, 2))
    if fmt == "e4m3":
        words = by_word.astype(ml_dtypes.float8_e4m3fn).view(np.uint8)
    else:
        c = by_word.astype(ml_dtypes.float4_e2m1fn).view(np.uint8) & 0xF
        words = c[..., 0::2] | (c[..., 1::2] << 4)
    return np.ascontiguousarray(words), np.ascontiguousarray(byte.astype(np.uint8).reshape(k // 512, 16, n))


def unpack_weight(words, scales, fmt):
    g, p, n, _ = words.shape
    if fmt == "e4m3":
        vals = np.ascontiguousarray(words).view(ml_dtypes.float8_e4m3fn).astype(np.float64)
    else:
        nib = np.empty((g, p, n, 4), np.uint8)
        nib[..., 0::2] = words & 0xF
        nib[..., 1::2] = words >> 4
        vals = E2M1[nib]
    vals = vals * np.repeat(np.exp2(scales.astype(np.float64) - 127.0), 8, axis=1)[..., None]
    return vals.transpose(0, 1, 3, 2).reshape(g * 512, n)

def planes(Y):
    n, m = Y.shape
    b = f64(bf(Y)).reshape(n // 32, 32, m)
    amax = np.abs(b).max(1)
    byte = np.clip(np.where(amax > 0, np.frexp(amax)[1] - 1 + 127 - 7, 1), 1, 254)
    codes = (b * np.exp2(127.0 - byte)[:, None, :]).reshape(n, m).astype(np.float32).astype(ml_dtypes.float8_e4m3fn).view(np.uint8)
    words = codes.reshape(n // 512, 128, 4, m).transpose(0, 1, 3, 2)
    return np.ascontiguousarray(words), np.ascontiguousarray(byte.astype(np.uint8).reshape(n // 512, 16, m))


B, D, K, N = 1024, 1024, 32, 16
M = K * N


def _quantile_huber_slope(d, tau):
    below = np.where(d < 0.0, 1.0, 0.0)
    weight = np.abs(tau[None, None, :, None] - below)
    return weight * np.minimum(np.maximum(d, -1.0), 1.0)


def setup_inputs():
    s, s2 = mx_kscale(D), mx_kscale(D)
    u = mx_kscale(B)
    common = np.random.standard_normal((D, K, 1))
    spread = np.random.standard_normal((D, K, N))
    wt = (1.1 * common + 0.5 * spread).reshape(D, M) / np.sqrt(D)
    h = bf(np.random.standard_normal((B, D)) * s)
    hn = bf(np.random.standard_normal((B, D)) * s2)
    w_words, w_scales = pack_weight(np.random.standard_normal((D, M)) * 0.7 / np.sqrt(D) / s[:, None], "e4m3")
    wt_words, wt_scales = pack_weight(wt / s2[:, None], "e4m3")
    return {
        "h": h,
        "hn": hn,
        "w_words": w_words,
        "w_scales": w_scales,
        "wt_words": wt_words,
        "wt_scales": wt_scales,
        "r": bf(np.random.standard_normal(B) * 0.5),
        "a": bf(np.random.uniform(0.5, 1.5, B) * u),
        "c": bf((1.0 + 0.1 * np.random.standard_normal(B)) / u),
    }


def core(h, hn, w_words, w_scales, wt_words, wt_scales, r, a, c):
    h, hn, r, a, c = f64(h), f64(hn), f64(r), f64(a), f64(c)
    w = unpack_weight(w_words, w_scales, "e4m3")
    wt = unpack_weight(wt_words, wt_scales, "e4m3")
    batch = h.shape[0]
    cols = w.shape[1]

    theta = (mxq(h, 1, "e4m3") @ w).reshape(batch, K, N)

    y = (r[:, None] + 0.97 * (mxq(hn, 1, "e4m3") @ wt)).reshape(batch, K, N)

    d = y[:, :, None, :] - theta[:, :, :, None]
    tau = (np.arange(N) + 0.5) / N

    e = -(batch ** -0.5) * np.mean(_quantile_huber_slope(d, tau), axis=-1)
    e = e.reshape(batch, cols)

    return mxq(h * a[:, None], 0, "e4m3").T @ mxq(e * c[:, None], 0, "e4m3")


def reference(h, hn, w_words, w_scales, wt_words, wt_scales, r, a, c):
    R_out = core(h, hn, w_words, w_scales, wt_words, wt_scales, r, a, c)
    words, scales = planes(R_out)
    return R_out, words, scales

@@ -1,0 +1,411 @@
+from contextlib import ExitStack
+
+import concourse.mybir as mybir
+from concourse.masks import make_identity
+
+B, D, K, N = 1024, 1024, 32, 16
+M = K * N
+FLOPS = 3 * 2 * B * D * M
+
+F32 = mybir.dt.float32
+BF16 = mybir.dt.bfloat16
+U32 = mybir.dt.uint32
+I32 = mybir.dt.int32
+U8 = mybir.dt.uint8
+FP8X4 = mybir.dt.float8_e4m3fn_x4
+ALU = mybir.AluOpType
+ACT = mybir.ActivationFunctionType
+
+P = 128
+PACK = 4
+GROUPS = 2
+UNITS = 4
+QUANTS = N // UNITS
+LANES = 32
+QUARTER = 128
+HALF = 256
+GAMMA = 0.97
+E_SCALE = B ** -0.5 / N / 2
+
+PHASES = [(0, 0, 2, 0), (0, 2, 2, 0), (1, 0, 2, 0), (1, 2, 2, 0),
+          (0, 0, 4, 256), (1, 0, 4, 256), (0, 0, 4, 384), (1, 0, 4, 384)]
+
+
+def tile_ensemblequantilehuberheadweightgrad_x2_kernel(
+    tc, h, hn, w_words, w_scales, wt_words, wt_scales, r, a, c, out_0, out_1, out_2
+):
+    nc = tc.nc
+    with ExitStack() as ctx:
+        keep = ctx.enter_context(tc.tile_pool(name="keep", bufs=1))
+        work = ctx.enter_context(tc.tile_pool(name="work", bufs=2))
+        psum = ctx.enter_context(tc.psum_pool(name="psum", bufs=2))
+        ctx.enter_context(tc.manual_schedule())
+
+        feats = {"h": h, "hn": hn}
+        words_in = {"h": w_words, "hn": wt_words}
+        scales_in = {"h": w_scales, "hn": wt_scales}
+        rows, w_codes, w_planes, w_stage = {}, {}, {}, {}
+
+        def load_rows(op, g, pair):
+            t = keep.tile([P, 2, D], BF16, name="rows_%s_%d_%d" % (op, g, pair), align_bytes=256)
+            view = feats[op].rearrange("(g p t) f -> g p t f", g=GROUPS, t=PACK)
+            nc.sync.dma_start(out=t[:], in_=view[g][:, 2 * pair : 2 * pair + 2, :])
+            rows[op, g, pair] = t
+
+        def load_weight(op, half):
+            t = keep.tile([P, GROUPS, HALF], U32, name="w_%s_%d" % (op, half), align_bytes=256)
+            view = words_in[op].rearrange("g p n t -> p g (n t)")
+            nc.sync.dma_start(
+                out=t[:].bitcast(I32),
+                in_=view[:, :, half * HALF * PACK : (half + 1) * HALF * PACK].bitcast(I32),
+            )
+            w_codes[op, half] = t
+
+        def load_weight_scales(op):
+            t = keep.tile([PACK, GROUPS * 4, M // 4], I32, name="wstage_%s" % op, align_bytes=64)
+            view = scales_in[op].rearrange("g (q r) n -> r (g q) n", r=4)
+            nc.scalar.dma_start(out=t[:], in_=view.bitcast(I32))
+            w_stage[op] = t
+
+        def load_vector(name, vec, queue):
+            t = keep.tile([P, GROUPS, PACK], BF16, name=name, align_bytes=64)
+            queue.dma_start(out=t[:], in_=vec.rearrange("(g p t) -> p g t", g=GROUPS, t=PACK))
+            return t
+
+        def spread_weight_scales(op):
+            plane = keep.tile([P, GROUPS, M], U8, name="wplane_%s" % op, align_bytes=64)
+            stage = w_stage[op][:].rearrange("r (g q) n -> r q g n", q=4)
+            for q in range(4):
+                nc.vector.tensor_copy(out=plane[32 * q : 32 * q + 4, :, :].bitcast(I32), in_=stage[:, q])
+            w_planes[op] = plane
+
+        load_rows("h", 0, 0)
+        load_weight_scales("h")
+        load_rows("hn", 0, 0)
+        load_weight_scales("hn")
+        c_sb = load_vector("c_sb", c, nc.scalar)
+        load_weight("h", 0)
+        load_weight("hn", 0)
+        a_sb = load_vector("a_sb", a, nc.sync)
+        r_sb = load_vector("r_sb", r, nc.sync)
+        load_rows("h", 0, 1)
+        load_rows("hn", 0, 1)
+        for pair in range(2):
+            load_rows("h", 1, pair)
+            load_rows("hn", 1, pair)
+        load_weight("h", 1)
+        load_weight("hn", 1)
+
+        ident = keep.tile([P, P], F32, name="ident", align_bytes=64)
+        make_identity(nc, ident[:])
+
+        factor = keep.tile([P, GROUPS, N, PACK], F32, name="factor", align_bytes=64)
+        for low, sign in ((0, 1.0), (N // 2, -1.0)):
+            nc.scalar.activation(
+                out=factor[:, :, low : low + N // 2, :],
+                in_=c_sb[:].unsqueeze(2).broadcast_to([P, GROUPS, N // 2, PACK]),
+                func=ACT.Copy,
+                scale=sign * E_SCALE,
+            )
+
+        turned, staged, f_codes, f_planes = {}, {}, {}, {}
+
+        def turn(op, g, pair, tag):
+            for s in range(2):
+                bank = psum.tile([P, GROUPS, 2, P], F32, name="turn", tag=tag)
+                words = rows[op, g, pair][:, s, :].bitcast(F32)
+                for kg in range(GROUPS):
+                    for u in range(2):
+                        nc.tensor.transpose(bank[:, kg, u, :], words[:, 256 * kg + u : 256 * (kg + 1) : 2], ident[:])
+                turned[op, g, pair, s] = bank
+
+        def unturn(op, g, pair, movers):
+            t = work.tile([P, 2, GROUPS, P, 2], F32, name="staged", align_bytes=64)
+            for s in range(2):
+                movers[s](out=t[:, s], in_=turned[op, g, pair, s][:].rearrange("p kg u b -> p kg b u"))
+            staged[op, g, pair] = t
+
+        def quantize_turned(op, g, pair):
+            codes = keep.tile([P, 2, GROUPS, P], U32, name="fc_%s_%d_%d" % (op, g, pair), align_bytes=64)
+            plane = keep.tile([P, 2, GROUPS, P], U8, name="fp_%s_%d_%d" % (op, g, pair), align_bytes=64)
+            nc.vector.quantize_mx(
+                out=codes[:].rearrange("p s g b -> p (s g b)").bitcast(FP8X4),
+                scales=plane[:].rearrange("p s g b -> p (s g b)"),
+                in_=staged[op, g, pair][:].rearrange("p s g b u -> p (s g b u)").bitcast(BF16),
+            )
+            f_codes[op, g, pair], f_planes[op, g, pair] = codes, plane
+
+        heads, targets = {}, {}
+
+        def head_matmuls(ph):
+            g, first, slots, col0 = PHASES[ph]
+            width = M // slots
+            half, low = divmod(col0, HALF)
+            for op, bufs in (("hn", 1), ("h", 2)):
+                bank = psum.tile([P, slots, width], F32, name="head_" + op, bufs=bufs)
+                for s in range(slots):
+                    pair, sl = divmod(first + s, 2)
+                    for kg in range(GROUPS):
+                        nc.tensor.matmul_mx(
+                            out=bank[:, s, :],
+                            lhsT=f_codes[op, g, pair][:, sl, kg, :].bitcast(FP8X4),
+                            lhsT_scale=f_planes[op, g, pair][:, sl, kg, :],
+                            rhs=w_codes[op, half][:, kg, low : low + width].bitcast(FP8X4),
+                            rhs_scale=w_planes[op][:, kg, col0 : col0 + width],
+                            start=(kg == 0),
+                            stop=(kg == GROUPS - 1),
+                        )
+                heads[op, ph] = bank
+
+        def make_targets(ph):
+            g, first, slots, col0 = PHASES[ph]
+            y = work.tile([P, N, slots, LANES // slots], F32, name="y", align_bytes=64)
+            for s in range(slots):
+                nc.scalar.activation(
+                    out=y[:, :, s, :],
+                    in_=heads["hn", ph][:, s, :].rearrange("p (k j) -> p j k", j=N),
+                    func=ACT.Identity,
+                    scale=GAMMA,
+                    bias=r_sb[:, g, first + s : first + s + 1],
+                )
+            targets[ph] = y
+
+        clipped, folded, sums, sums_sb, backs = {}, {}, {}, {}, {}
+
+        def differences(n):
+            ph, u = divmod(n, UNITS)
+            shape = [P, N, QUANTS, LANES]
+            theta = heads["h", ph][:].rearrange("p s w -> p (s w)").rearrange("p (l i) -> p i l", i=N)[:, QUANTS * u : QUANTS * (u + 1), :]
+            theta = theta.unsqueeze(1).broadcast_to(shape)
+            y = targets[ph][:].rearrange("p j s k -> p j (s k)").unsqueeze(2).broadcast_to(shape)
+            d = work.tile(shape, F32, name="d", align_bytes=64)
+            if u < UNITS // 2:
+                nc.vector.tensor_tensor(out=d[:], in0=theta, in1=y, op=ALU.subtract)
+            else:
+                nc.vector.tensor_tensor(out=d[:], in0=y, in1=theta, op=ALU.subtract)
+            return d
+
+        def clip(n, d):
+            t = work.tile([P, N, QUANTS, LANES], F32, name="clipped", bufs=4, align_bytes=64)
+            nc.gpsimd.tensor_scalar(
+                out=t[:].rearrange("p j i l -> p (j i l)"),
+                in0=d[:].rearrange("p j i l -> p (j i l)"),
+                scalar1=1.0, scalar2=-1.0, op0=ALU.min, op1=ALU.max,
+            )
+            clipped[n] = t
+
+        def fold(n):
+            u = n % UNITS
+            t = work.tile([P, N, QUANTS, LANES], F32, name="folded", bufs=3, align_bytes=64)
+            for i in range(QUANTS):
+                slope = abs(2 * (QUANTS * u + i) + 1 - N) / N
+                nc.scalar.activation(out=t[:, :, i, :], in_=clipped[n][:, :, i, :], func=ACT.Abs, scale=slope)
+            folded[n] = t
+
+        def add_up(n):
+            ph, u = divmod(n, UNITS)
+            if u == 0:
+                sums[ph] = psum.tile([P, UNITS, P], F32, name="sums", tag="sums")
+            for j in range(N):
+                for second, src in enumerate((clipped[n], folded[n])):
+                    nc.tensor.matmul(
+                        out=sums[ph][:, u, :],
+                        lhsT=src[:, j].rearrange("p i l -> p (i l)"),
+                        rhs=ident[:],
+                        is_transpose=True,
+                        start=(j == 0 and second == 0),
+                        stop=(j == N - 1 and second == 1),
+                    )
+
+        def sums_out(ph):
+            t = work.tile([P, UNITS, P], F32, name="sums_sb", align_bytes=64)
+            nc.scalar.copy(out=t[:], in_=sums[ph][:])
+            sums_sb[ph] = t
+
+        def turn_back(ph):
+            bank = psum.tile([P, UNITS, P], F32, name="back", bufs=1)
+            for u in range(UNITS):
+                nc.tensor.transpose(bank[:, u, :], sums_sb[ph][:, u, :], ident[:])
+            backs[ph] = bank
+
+        e_bf, e_codes, e_planes = {}, {}, {}
+
+        def weigh(ph):
+            g, first, slots, col0 = PHASES[ph]
+            members = LANES // slots
+            if first == 0:
+                e_bf[g, col0] = keep.tile([P, members, N, PACK], BF16, name="e_%d_%d" % (g, col0), align_bytes=64)
+            nc.vector.tensor_tensor(
+                out=e_bf[g, col0][:, :, :, first : first + slots],
+                in0=backs[ph][:].rearrange("p u l -> p (u l)").rearrange("p (i s k) -> p k i s", i=N, s=slots),
+                in1=factor[:, g, :, first : first + slots].unsqueeze(1).broadcast_to([P, members, N, slots]),
+                op=ALU.mult,
+            )
+
+        def quantize_e(ph):
+            g, first, slots, col0 = PHASES[ph]
+            width = M // slots
+            codes = keep.tile([P, width], U32, name="ec_%d_%d" % (g, col0), align_bytes=64)
+            plane = keep.tile([P, width], U8, name="ep_%d_%d" % (g, col0), align_bytes=64)
+            nc.vector.quantize_mx(
+                out=codes[:].bitcast(FP8X4),
+                scales=plane[:],
+                in_=e_bf[g, col0][:].rearrange("p k i t -> p (k i t)"),
+            )
+            for low in range(0, width, QUARTER):
+                e_codes[g, (col0 + low) // QUARTER] = codes[:, low : low + QUARTER]
+                e_planes[g, (col0 + low) // QUARTER] = plane[:, low : low + QUARTER]
+
+        scaled, laid, ha_codes, ha_planes = {}, {}, {}, {}
+
+        def scale_rows(g, t):
+            if t == 0:
+                scaled[g] = work.tile([P, PACK, D], BF16, name="scaled", bufs=1, align_bytes=64)
+            nc.vector.tensor_scalar(
+                out=scaled[g][:, t, :], in0=rows["h", g, t // 2][:, t % 2, :],
+                scalar1=a_sb[:, g, t : t + 1], scalar2=None, op0=ALU.mult,
+            )
+
+        def lay_rows(g, fg):
+            t = work.tile([P, PACK, P, PACK], BF16, name="laid", align_bytes=64)
+            nc.vector.tensor_copy(
+                out=t[:],
+                in_=scaled[g][:, :, 512 * fg : 512 * (fg + 1)].rearrange("p t (m v) -> p v m t", v=PACK),
+            )
+            laid[g, fg] = t
+
+        def quantize_laid(g, fg):
+            codes = keep.tile([P, PACK, P], U32, name="hc_%d_%d" % (g, fg), align_bytes=64)
+            plane = keep.tile([P, PACK, P], U8, name="hp_%d_%d" % (g, fg), align_bytes=64)
+            nc.vector.quantize_mx(
+                out=codes[:].rearrange("p v m -> p (v m)").bitcast(FP8X4),
+                scales=plane[:].rearrange("p v m -> p (v m)"),
+                in_=laid[g, fg][:].rearrange("p v m t -> p (v m t)"),
+            )
+            ha_codes[g, fg], ha_planes[g, fg] = codes, plane
+
+        grads, grads_bf = {}, {}
+
+        def grad_matmuls(q):
+            for fg in range(GROUPS):
+                bank = psum.tile([P, PACK, QUARTER], F32, name="grad", tag="aux")
+                for v in range(PACK):
+                    for g in range(GROUPS):
+                        nc.tensor.matmul_mx(
+                            out=bank[:, v, :],
+                            lhsT=ha_codes[g, fg][:, v, :].bitcast(FP8X4),
+                            lhsT_scale=ha_planes[g, fg][:, v, :],
+                            rhs=e_codes[g, q].bitcast(FP8X4),
+                            rhs_scale=e_planes[g, q],
+                            start=(g == 0),
+                            stop=(g == GROUPS - 1),
+                        )
+                grads[q, fg] = bank
+
+        def store_grad(q, fg):
+            t = work.tile([P, PACK, QUARTER], F32, name="grad_sb", bufs=4, align_bytes=64)
+            nc.scalar.copy(out=t[:], in_=grads[q, fg][:])
+            view = out_0.rearrange("(g p v) m -> g p v m", g=GROUPS, v=PACK)
+            nc.sync.dma_start(out=view[fg][:, :, q * QUARTER : (q + 1) * QUARTER], in_=t[:])
+
+        def round_grad(q, fg):
+            if q not in grads_bf:
+                grads_bf[q] = work.tile([P, GROUPS, QUARTER, PACK], BF16, name="grad_bf", align_bytes=64)
+            nc.vector.tensor_copy(out=grads_bf[q][:, fg], in_=grads[q, fg][:].rearrange("p v m -> p m v"))
+
+        def grad_out(q):
+            store_grad(q, 0)
+            round_grad(q, 1)
+            store_grad(q, 1)
+            round_grad(q, 0)
+
+        def store_planes(q):
+            codes = work.tile([P, GROUPS, QUARTER], U32, name="out_codes", align_bytes=64)
+            plane = work.tile([P, GROUPS, QUARTER], U8, name="out_plane", align_bytes=64)
+            nc.vector.quantize_mx(
+                out=codes[:].rearrange("p g m -> p (g m)").bitcast(FP8X4),
+                scales=plane[:].rearrange("p g m -> p (g m)"),
+                in_=grads_bf[q][:].rearrange("p g m v -> p (g m v)"),
+            )
+            word_view = out_1.rearrange("g p m t -> p g (m t)")
+            nc.sync.dma_start(
+                out=word_view[:, :, q * QUARTER * PACK : (q + 1) * QUARTER * PACK].bitcast(I32),
+                in_=codes[:].bitcast(I32),
+            )
+            scale_view = out_2.rearrange("g s m -> s g m")
+            for quad in range(4):
+                nc.sync.dma_start(
+                    out=scale_view[4 * quad : 4 * quad + 4, :, q * QUARTER : (q + 1) * QUARTER].bitcast(I32),
+                    in_=plane[32 * quad : 32 * quad + 4, :, :].bitcast(I32),
+                )
+
+        both = (nc.scalar.copy, nc.vector.tensor_copy)
+        scalar_only = (nc.scalar.copy, nc.scalar.copy)
+
+        turn("h", 0, 0, "aux")
+        turn("hn", 0, 0, "sums")
+        spread_weight_scales("h")
+        spread_weight_scales("hn")
+        unturn("h", 0, 0, both)
+        scale_rows(0, 0)
+        quantize_turned("h", 0, 0)
+        unturn("hn", 0, 0, both)
+        scale_rows(0, 1)
+        quantize_turned("hn", 0, 0)
+        head_matmuls(0)
+        make_targets(0)
+        turn("h", 0, 1, "aux")
+        scale_rows(0, 2)
+        scale_rows(0, 3)
+
+        port, vector_side, scalar_side, tensor_side = {}, {}, {}, {}
+
+        def at(table, step, fn, *args):
+            table.setdefault(step, []).append((fn, args))
+
+        for ph in range(1, 4):
+            g, pair = divmod(ph, 2)
+            if ph > 1:
+                at(tensor_side, 4 * ph - 5, turn, "h", g, pair, "aux")
+            at(scalar_side, 4 * ph - 4, unturn, "h", g, pair, scalar_only)
+            at(tensor_side, 4 * ph - 4, turn, "hn", g, pair, "aux")
+            at(scalar_side, 4 * ph - 3, unturn, "hn", g, pair, scalar_only)
+            at(port, 4 * ph - 3, quantize_turned, "h", g, pair)
+            at(port, 4 * ph - 2, quantize_turned, "hn", g, pair)
+        for ph in range(len(PHASES)):
+            if ph > 0:
+                at(tensor_side, 4 * ph - 2, head_matmuls, ph)
+                at(scalar_side, 4 * ph - 1, make_targets, ph)
+            at(scalar_side, 4 * ph + 7, sums_out, ph)
+            at(tensor_side, 4 * ph + 7, turn_back, ph)
+            at(vector_side, 4 * ph + 8, weigh, ph)
+            if PHASES[ph][1] + PHASES[ph][2] == PACK:
+                at(port, 4 * ph + 9, quantize_e, ph)
+        for step, fn, args in (
+            (0, lay_rows, (0, 0)), (3, lay_rows, (0, 1)), (4, quantize_laid, (0, 0)), (7, quantize_laid, (0, 1)),
+            (8, scale_rows, (1, 0)), (11, scale_rows, (1, 1)), (12, scale_rows, (1, 2)), (14, scale_rows, (1, 3)),
+            (15, lay_rows, (1, 0)), (16, lay_rows, (1, 1)), (17, quantize_laid, (1, 0)), (18, quantize_laid, (1, 1)),
+        ):
+            at(port, step, fn, *args)
+        for q, step in enumerate((22, 26, 30, 38)):
+            at(tensor_side, step, grad_matmuls, q)
+            at(vector_side, step + 1, grad_out, q)
+            at(port, step + 2, store_planes, q)
+
+        units = UNITS * len(PHASES)
+        for step in range(units + 9):
+            if step < units:
+                d = differences(step)
+            for fn, args in port.get(step, []):
+                fn(*args)
+            if step < units:
+                clip(step, d)
+            if 2 <= step < units + 2:
+                fold(step - 2)
+            for table in (vector_side, scalar_side):
+                for fn, args in table.get(step, []):
+                    fn(*args)
+            if 3 <= step < units + 3:
+                add_up(step - 3)
+            for fn, args in tensor_side.get(step, []):
+                fn(*args)

@@ -15,6 +15,7 @@ U8 = mybir.dt.uint8
 FP8X4 = mybir.dt.float8_e4m3fn_x4
 ALU = mybir.AluOpType
 ACT = mybir.ActivationFunctionType
+AXIS_X = mybir.AxisListType.X
 
 P = 128
 PACK = 4
@@ -29,6 +30,9 @@ E_SCALE = B ** -0.5 / N / 2
 
 PHASES = [(0, 0, 2, 0), (0, 2, 2, 0), (1, 0, 2, 0), (1, 2, 2, 0),
           (0, 0, 4, 256), (1, 0, 4, 256), (0, 0, 4, 384), (1, 0, 4, 384)]
+
+
+REDUCED = (6, 14, 22, 30)
 
 
 def tile_ensemblequantilehuberheadweightgrad_x2_kernel(
@@ -86,7 +90,7 @@ def tile_ensemblequantilehuberheadweightgrad_x2_kernel(
         c_sb = load_vector("c_sb", c, nc.scalar)
         load_weight("h", 0)
         load_weight("hn", 0)
-        a_sb = load_vector("a_sb", a, nc.sync)
+        a_bf = load_vector("a_bf", a, nc.sync)
         r_sb = load_vector("r_sb", r, nc.sync)
         load_rows("h", 0, 1)
         load_rows("hn", 0, 1)
@@ -107,6 +111,8 @@ def tile_ensemblequantilehuberheadweightgrad_x2_kernel(
                 func=ACT.Copy,
                 scale=sign * E_SCALE,
             )
+
+        a_sb = keep.tile([P, GROUPS, PACK], F32, name="a_sb", align_bytes=64)
 
         turned, staged, f_codes, f_planes = {}, {}, {}, {}
 
@@ -135,27 +141,26 @@ def tile_ensemblequantilehuberheadweightgrad_x2_kernel(
             )
             f_codes[op, g, pair], f_planes[op, g, pair] = codes, plane
 
-        heads, targets = {}, {}
+        heads, targets, target_rows = {}, {}, {}
 
-        def head_matmuls(ph):
+        def head_matmuls(op, ph, part):
             g, first, slots, col0 = PHASES[ph]
             width = M // slots
             half, low = divmod(col0, HALF)
-            for op, bufs in (("hn", 1), ("h", 2)):
-                bank = psum.tile([P, slots, width], F32, name="head_" + op, bufs=bufs)
-                for s in range(slots):
-                    pair, sl = divmod(first + s, 2)
-                    for kg in range(GROUPS):
-                        nc.tensor.matmul_mx(
-                            out=bank[:, s, :],
-                            lhsT=f_codes[op, g, pair][:, sl, kg, :].bitcast(FP8X4),
-                            lhsT_scale=f_planes[op, g, pair][:, sl, kg, :],
-                            rhs=w_codes[op, half][:, kg, low : low + width].bitcast(FP8X4),
-                            rhs_scale=w_planes[op][:, kg, col0 : col0 + width],
-                            start=(kg == 0),
-                            stop=(kg == GROUPS - 1),
-                        )
-                heads[op, ph] = bank
+            if part == 0:
+                heads[op, ph] = psum.tile([P, slots, width], F32, name="head_" + op, bufs=2 if op == "h" else 1)
+            for s in range(part * slots // 2, (part + 1) * slots // 2):
+                pair, sl = divmod(first + s, 2)
+                for kg in range(GROUPS):
+                    nc.tensor.matmul_mx(
+                        out=heads[op, ph][:, s, :],
+                        lhsT=f_codes[op, g, pair][:, sl, kg, :].bitcast(FP8X4),
+                        lhsT_scale=f_planes[op, g, pair][:, sl, kg, :],
+                        rhs=w_codes[op, half][:, kg, low : low + width].bitcast(FP8X4),
+                        rhs_scale=w_planes[op][:, kg, col0 : col0 + width],
+                        start=(kg == 0),
+                        stop=(kg == GROUPS - 1),
+                    )
 
         def make_targets(ph):
             g, first, slots, col0 = PHASES[ph]
@@ -169,15 +174,29 @@ def tile_ensemblequantilehuberheadweightgrad_x2_kernel(
                     bias=r_sb[:, g, first + s : first + s + 1],
                 )
             targets[ph] = y
+            if any(n // UNITS == ph for n in REDUCED):
+                y = work.tile([P, slots, LANES // slots * N], F32, name="y_rows", bufs=1, align_bytes=64)
+                for s in range(slots):
+                    nc.scalar.activation(
+                        out=y[:, s, :], in_=heads["hn", ph][:, s, :], func=ACT.Identity,
+                        scale=GAMMA, bias=r_sb[:, g, first + s : first + s + 1],
+                    )
+                target_rows[ph] = y
 
         clipped, folded, sums, sums_sb, backs = {}, {}, {}, {}, {}
 
         def differences(n):
             ph, u = divmod(n, UNITS)
-            shape = [P, N, QUANTS, LANES]
             theta = heads["h", ph][:].rearrange("p s w -> p (s w)").rearrange("p (l i) -> p i l", i=N)[:, QUANTS * u : QUANTS * (u + 1), :]
-            theta = theta.unsqueeze(1).broadcast_to(shape)
-            y = targets[ph][:].rearrange("p j s k -> p j (s k)").unsqueeze(2).broadcast_to(shape)
+            if n in REDUCED:
+                shape = [P, QUANTS, LANES, N]
+                theta = theta.unsqueeze(3).broadcast_to(shape)
+                y = target_rows[ph][:].rearrange("p s w -> p (s w)").rearrange("p (l j) -> p l j", j=N)
+                y = y.unsqueeze(1).broadcast_to(shape)
+            else:
+                shape = [P, N, QUANTS, LANES]
+                theta = theta.unsqueeze(1).broadcast_to(shape)
+                y = targets[ph][:].rearrange("p j s k -> p j (s k)").unsqueeze(2).broadcast_to(shape)
             d = work.tile(shape, F32, name="d", align_bytes=64)
             if u < UNITS // 2:
                 nc.vector.tensor_tensor(out=d[:], in0=theta, in1=y, op=ALU.subtract)
@@ -186,35 +205,54 @@ def tile_ensemblequantilehuberheadweightgrad_x2_kernel(
             return d
 
         def clip(n, d):
-            t = work.tile([P, N, QUANTS, LANES], F32, name="clipped", bufs=4, align_bytes=64)
+            t = work.tile(list(d.shape), F32, name="clipped", bufs=4, align_bytes=64)
             nc.gpsimd.tensor_scalar(
-                out=t[:].rearrange("p j i l -> p (j i l)"),
-                in0=d[:].rearrange("p j i l -> p (j i l)"),
+                out=t[:].rearrange("p x y z -> p (x y z)"),
+                in0=d[:].rearrange("p x y z -> p (x y z)"),
                 scalar1=1.0, scalar2=-1.0, op0=ALU.min, op1=ALU.max,
             )
             clipped[n] = t
 
+        reduced = {}
+
+        def reduce_over_j(n, absolute):
+            t = work.tile([P, 1, QUANTS, LANES], F32, name="reduced", align_bytes=64)
+            out = t[:].rearrange("p o i l -> p (o i l)")
+            terms = clipped[n][:].rearrange("p i l j -> p (i l) j")
+            if absolute:
+                nc.vector.tensor_reduce(out=out, in_=terms, axis=AXIS_X, op=ALU.add, apply_absolute_value=True)
+            else:
+                nc.vector.tensor_reduce(out=out, in_=terms, axis=AXIS_X, op=ALU.add)
+            reduced[n, absolute] = t
+
         def fold(n):
             u = n % UNITS
-            t = work.tile([P, N, QUANTS, LANES], F32, name="folded", bufs=3, align_bytes=64)
+            if n in REDUCED:
+                src = reduced[n, True]
+                t = work.tile([P, 1, QUANTS, LANES], F32, name="folded_sum", bufs=1, align_bytes=64)
+            else:
+                src = clipped[n]
+                t = work.tile([P, N, QUANTS, LANES], F32, name="folded", bufs=3, align_bytes=64)
             for i in range(QUANTS):
                 slope = abs(2 * (QUANTS * u + i) + 1 - N) / N
-                nc.scalar.activation(out=t[:, :, i, :], in_=clipped[n][:, :, i, :], func=ACT.Abs, scale=slope)
+                nc.scalar.activation(out=t[:, :, i, :], in_=src[:, :, i, :], func=ACT.Abs, scale=slope)
             folded[n] = t
 
         def add_up(n):
             ph, u = divmod(n, UNITS)
             if u == 0:
                 sums[ph] = psum.tile([P, UNITS, P], F32, name="sums", tag="sums")
-            for j in range(N):
-                for second, src in enumerate((clipped[n], folded[n])):
+            plain = reduced[n, False] if n in REDUCED else clipped[n]
+            terms = plain.shape[1]
+            for j in range(terms):
+                for second, src in enumerate((plain, folded[n])):
                     nc.tensor.matmul(
                         out=sums[ph][:, u, :],
                         lhsT=src[:, j].rearrange("p i l -> p (i l)"),
                         rhs=ident[:],
                         is_transpose=True,
                         start=(j == 0 and second == 0),
-                        stop=(j == N - 1 and second == 1),
+                        stop=(j == terms - 1 and second == 1),
                     )
 
         def sums_out(ph):
@@ -260,17 +298,21 @@ def tile_ensemblequantilehuberheadweightgrad_x2_kernel(
 
         def scale_rows(g, t):
             if t == 0:
-                scaled[g] = work.tile([P, PACK, D], BF16, name="scaled", bufs=1, align_bytes=64)
-            nc.vector.tensor_scalar(
-                out=scaled[g][:, t, :], in0=rows["h", g, t // 2][:, t % 2, :],
-                scalar1=a_sb[:, g, t : t + 1], scalar2=None, op0=ALU.mult,
-            )
+                scaled[g] = work.tile([P, PACK, D], BF16, name="scaled", align_bytes=64)
+            src = rows["h", g, t // 2][:, t % 2, :]
+            if g == 0:
+                nc.vector.tensor_scalar(
+                    out=scaled[g][:, t, :], in0=src, scalar1=a_sb[:, g, t : t + 1], scalar2=None, op0=ALU.mult
+                )
+            else:
+                nc.scalar.activation(out=scaled[g][:, t, :], in_=src, func=ACT.Copy, scale=a_sb[:, g, t : t + 1])
 
         def lay_rows(g, fg):
             t = work.tile([P, PACK, P, PACK], BF16, name="laid", align_bytes=64)
-            nc.vector.tensor_copy(
+            nc.gpsimd.tensor_scalar(
                 out=t[:],
-                in_=scaled[g][:, :, 512 * fg : 512 * (fg + 1)].rearrange("p t (m v) -> p v m t", v=PACK),
+                in0=scaled[g][:, :, 512 * fg : 512 * (fg + 1)].rearrange("p t (m v) -> p v m t", v=PACK),
+                scalar1=1.0, scalar2=0.0, op0=ALU.mult, op1=ALU.add,
             )
             laid[g, fg] = t
 
@@ -286,21 +328,21 @@ def tile_ensemblequantilehuberheadweightgrad_x2_kernel(
 
         grads, grads_bf = {}, {}
 
-        def grad_matmuls(q):
-            for fg in range(GROUPS):
-                bank = psum.tile([P, PACK, QUARTER], F32, name="grad", tag="aux")
-                for v in range(PACK):
-                    for g in range(GROUPS):
-                        nc.tensor.matmul_mx(
-                            out=bank[:, v, :],
-                            lhsT=ha_codes[g, fg][:, v, :].bitcast(FP8X4),
-                            lhsT_scale=ha_planes[g, fg][:, v, :],
-                            rhs=e_codes[g, q].bitcast(FP8X4),
-                            rhs_scale=e_planes[g, q],
-                            start=(g == 0),
-                            stop=(g == GROUPS - 1),
-                        )
-                grads[q, fg] = bank
+        def grad_matmuls(q, part):
+            fg, low = divmod(2 * part, PACK)
+            if low == 0:
+                grads[q, fg] = psum.tile([P, PACK, QUARTER], F32, name="grad", tag="aux")
+            for v in range(low, low + 2):
+                for g in range(GROUPS):
+                    nc.tensor.matmul_mx(
+                        out=grads[q, fg][:, v, :],
+                        lhsT=ha_codes[g, fg][:, v, :].bitcast(FP8X4),
+                        lhsT_scale=ha_planes[g, fg][:, v, :],
+                        rhs=e_codes[g, q].bitcast(FP8X4),
+                        rhs_scale=e_planes[g, q],
+                        start=(g == 0),
+                        stop=(g == GROUPS - 1),
+                    )
 
         def store_grad(q, fg):
             t = work.tile([P, PACK, QUARTER], F32, name="grad_sb", bufs=4, align_bytes=64)
@@ -308,16 +350,10 @@ def tile_ensemblequantilehuberheadweightgrad_x2_kernel(
             view = out_0.rearrange("(g p v) m -> g p v m", g=GROUPS, v=PACK)
             nc.sync.dma_start(out=view[fg][:, :, q * QUARTER : (q + 1) * QUARTER], in_=t[:])
 
-        def round_grad(q, fg):
+        def round_grad(q, fg, mover):
             if q not in grads_bf:
                 grads_bf[q] = work.tile([P, GROUPS, QUARTER, PACK], BF16, name="grad_bf", align_bytes=64)
-            nc.vector.tensor_copy(out=grads_bf[q][:, fg], in_=grads[q, fg][:].rearrange("p v m -> p m v"))
-
-        def grad_out(q):
-            store_grad(q, 0)
-            round_grad(q, 1)
-            store_grad(q, 1)
-            round_grad(q, 0)
+            mover(out=grads_bf[q][:, fg], in_=grads[q, fg][:].rearrange("p v m -> p m v"))
 
         def store_planes(q):
             codes = work.tile([P, GROUPS, QUARTER], U32, name="out_codes", align_bytes=64)
@@ -346,66 +382,88 @@ def tile_ensemblequantilehuberheadweightgrad_x2_kernel(
         turn("hn", 0, 0, "sums")
         spread_weight_scales("h")
         spread_weight_scales("hn")
+        nc.vector.tensor_copy(out=a_sb[:], in_=a_bf[:])
         unturn("h", 0, 0, both)
         scale_rows(0, 0)
         quantize_turned("h", 0, 0)
         unturn("hn", 0, 0, both)
         scale_rows(0, 1)
         quantize_turned("hn", 0, 0)
-        head_matmuls(0)
+        for op in ("h", "hn"):
+            for part in range(2):
+                head_matmuls(op, 0, part)
         make_targets(0)
         turn("h", 0, 1, "aux")
         scale_rows(0, 2)
         scale_rows(0, 3)
+        lay_rows(0, 0)
 
-        port, vector_side, scalar_side, tensor_side = {}, {}, {}, {}
+        port, vector_side, pool_side, scalar_side, tensor_side = {}, {}, {}, {}, {}
 
         def at(table, step, fn, *args):
             table.setdefault(step, []).append((fn, args))
 
-        for ph in range(1, 4):
-            g, pair = divmod(ph, 2)
-            if ph > 1:
-                at(tensor_side, 4 * ph - 5, turn, "h", g, pair, "aux")
-            at(scalar_side, 4 * ph - 4, unturn, "h", g, pair, scalar_only)
-            at(tensor_side, 4 * ph - 4, turn, "hn", g, pair, "aux")
-            at(scalar_side, 4 * ph - 3, unturn, "hn", g, pair, scalar_only)
-            at(port, 4 * ph - 3, quantize_turned, "h", g, pair)
-            at(port, 4 * ph - 2, quantize_turned, "hn", g, pair)
+        for op, g, pair, turn_at, quantize_at in (
+            ("h", 0, 1, -1, 1), ("hn", 0, 1, 0, 2), ("h", 1, 0, 1, 3), ("hn", 1, 0, 2, 4),
+            ("h", 1, 1, 4, 6), ("hn", 1, 1, 6, 9),
+        ):
+            at(tensor_side, turn_at, turn, op, g, pair, "aux")
+            at(scalar_side, turn_at + 1, unturn, op, g, pair, scalar_only)
+            at(port, quantize_at, quantize_turned, op, g, pair)
         for ph in range(len(PHASES)):
             if ph > 0:
-                at(tensor_side, 4 * ph - 2, head_matmuls, ph)
+                steps = (1, 1, 2, 2) if ph == 1 else range(4 * ph - 5, 4 * ph - 1)
+                for step, (op, part) in zip(steps, (("h", 0), ("h", 1), ("hn", 0), ("hn", 1))):
+                    at(tensor_side, step, head_matmuls, op, ph, part)
                 at(scalar_side, 4 * ph - 1, make_targets, ph)
             at(scalar_side, 4 * ph + 7, sums_out, ph)
             at(tensor_side, 4 * ph + 7, turn_back, ph)
             at(vector_side, 4 * ph + 8, weigh, ph)
             if PHASES[ph][1] + PHASES[ph][2] == PACK:
                 at(port, 4 * ph + 9, quantize_e, ph)
-        for step, fn, args in (
-            (0, lay_rows, (0, 0)), (3, lay_rows, (0, 1)), (4, quantize_laid, (0, 0)), (7, quantize_laid, (0, 1)),
-            (8, scale_rows, (1, 0)), (11, scale_rows, (1, 1)), (12, scale_rows, (1, 2)), (14, scale_rows, (1, 3)),
-            (15, lay_rows, (1, 0)), (16, lay_rows, (1, 1)), (17, quantize_laid, (1, 0)), (18, quantize_laid, (1, 1)),
-        ):
-            at(port, step, fn, *args)
-        for q, step in enumerate((22, 26, 30, 38)):
-            at(tensor_side, step, grad_matmuls, q)
-            at(vector_side, step + 1, grad_out, q)
-            at(port, step + 2, store_planes, q)
+        for n in REDUCED:
+            at(vector_side, n + 1, reduce_over_j, n, False)
+            at(vector_side, n + 2, reduce_over_j, n, True)
+            at(scalar_side, n + 3, fold, n)
+        for t, step in enumerate((8, 8, 11, 12)):
+            at(scalar_side, step, scale_rows, 1, t)
+        for step, g, fg in ((7, 0, 1), (15, 1, 0), (16, 1, 1)):
+            at(pool_side, step, lay_rows, g, fg)
+        for step, g, fg in ((5, 0, 0), (10, 0, 1), (18, 1, 0), (19, 1, 1)):
+            at(port, step, quantize_laid, g, fg)
+        for q, step in enumerate((22, 26, 30)):
+            for part in range(4):
+                at(tensor_side, step + part, grad_matmuls, q, part)
+            for fg in range(GROUPS):
+                at(scalar_side, step + 2 + 2 * fg, store_grad, q, fg)
+                at(scalar_side, step + 2 + 2 * fg, round_grad, q, fg, nc.scalar.copy)
+            at(port, step + 5, store_planes, q)
 
         units = UNITS * len(PHASES)
-        for step in range(units + 9):
+        for step in range(units + 6):
             if step < units:
                 d = differences(step)
             for fn, args in port.get(step, []):
                 fn(*args)
             if step < units:
                 clip(step, d)
-            if 2 <= step < units + 2:
+            if 2 <= step < units + 2 and step - 2 not in REDUCED:
                 fold(step - 2)
-            for table in (vector_side, scalar_side):
+            for table in (vector_side, pool_side, scalar_side):
                 for fn, args in table.get(step, []):
                     fn(*args)
-            if 3 <= step < units + 3:
+            if 3 <= step < units + 3 and step - 3 not in REDUCED:
                 add_up(step - 3)
+            if step - 4 in REDUCED:
+                add_up(step - 4)
             for fn, args in tensor_side.get(step, []):
                 fn(*args)
+
+        last = 3
+        for part in range(4):
+            grad_matmuls(last, part)
+        store_grad(last, 0)
+        round_grad(last, 1, nc.vector.tensor_copy)
+        store_grad(last, 1)
+        round_grad(last, 0, nc.vector.tensor_copy)
+        store_planes(last)

@@ -238,22 +238,28 @@ def tile_ensemblequantilehuberheadweightgrad_x2_kernel(
                 nc.scalar.activation(out=t[:, :, i, :], in_=src[:, :, i, :], func=ACT.Abs, scale=slope)
             folded[n] = t
 
-        def add_up(n):
+        def add_up(n, woven=()):
             ph, u = divmod(n, UNITS)
             if u == 0:
                 sums[ph] = psum.tile([P, UNITS, P], F32, name="sums", tag="sums")
             plain = reduced[n, False] if n in REDUCED else clipped[n]
             terms = plain.shape[1]
+            slots = {0: (), 1: (3,), 2: (1, 3)}[len(woven)]
             for j in range(terms):
+                slot = j // 4 if j % 4 == 3 else None
                 for second, src in enumerate((plain, folded[n])):
+                    as_product = second == 1 and slot is not None and slot not in slots
                     nc.tensor.matmul(
                         out=sums[ph][:, u, :],
                         lhsT=src[:, j].rearrange("p i l -> p (i l)"),
                         rhs=ident[:],
-                        is_transpose=True,
+                        is_transpose=not as_product,
                         start=(j == 0 and second == 0),
                         stop=(j == terms - 1 and second == 1),
                     )
+                if slot in slots:
+                    fn, args = woven[slots.index(slot)]
+                    fn(*args)
 
         def sums_out(ph):
             t = work.tile([P, UNITS, P], F32, name="sums_sb", align_bytes=64)
@@ -398,7 +404,7 @@ def tile_ensemblequantilehuberheadweightgrad_x2_kernel(
         scale_rows(0, 3)
         lay_rows(0, 0)
 
-        port, vector_side, pool_side, scalar_side, tensor_side = {}, {}, {}, {}, {}
+        port, vector_side, pool_side, scalar_side, tensor_side, weave = {}, {}, {}, {}, {}, {}
 
         def at(table, step, fn, *args):
             table.setdefault(step, []).append((fn, args))
@@ -414,7 +420,10 @@ def tile_ensemblequantilehuberheadweightgrad_x2_kernel(
             if ph > 0:
                 steps = (1, 1, 2, 2) if ph == 1 else range(4 * ph - 5, 4 * ph - 1)
                 for step, (op, part) in zip(steps, (("h", 0), ("h", 1), ("hn", 0), ("hn", 1))):
-                    at(tensor_side, step, head_matmuls, op, ph, part)
+                    if ph == 1:
+                        at(tensor_side, step, head_matmuls, op, ph, part)
+                    else:
+                        at(weave, step + 1 if step - 3 in REDUCED else step, head_matmuls, op, ph, part)
                 at(scalar_side, 4 * ph - 1, make_targets, ph)
             at(scalar_side, 4 * ph + 7, sums_out, ph)
             at(tensor_side, 4 * ph + 7, turn_back, ph)
@@ -431,13 +440,13 @@ def tile_ensemblequantilehuberheadweightgrad_x2_kernel(
             at(pool_side, step, lay_rows, g, fg)
         for step, g, fg in ((5, 0, 0), (10, 0, 1), (18, 1, 0), (19, 1, 1)):
             at(port, step, quantize_laid, g, fg)
-        for q, step in enumerate((22, 26, 30)):
+        for q, steps, planes_at in ((0, (22, 23, 24, 27), 30), (1, (27, 28, 29, 29), 31), (2, (30, 31, 32, 32), 34)):
             for part in range(4):
-                at(tensor_side, step + part, grad_matmuls, q, part)
+                at(weave, steps[part], grad_matmuls, q, part)
             for fg in range(GROUPS):
-                at(scalar_side, step + 2 + 2 * fg, store_grad, q, fg)
-                at(scalar_side, step + 2 + 2 * fg, round_grad, q, fg, nc.scalar.copy)
-            at(port, step + 5, store_planes, q)
+                at(scalar_side, steps[2 * fg + 1] + 1, store_grad, q, fg)
+                at(scalar_side, steps[2 * fg + 1] + 1, round_grad, q, fg, nc.scalar.copy)
+            at(port, planes_at, store_planes, q)
 
         units = UNITS * len(PHASES)
         for step in range(units + 6):
@@ -453,7 +462,7 @@ def tile_ensemblequantilehuberheadweightgrad_x2_kernel(
                 for fn, args in table.get(step, []):
                     fn(*args)
             if 3 <= step < units + 3 and step - 3 not in REDUCED:
-                add_up(step - 3)
+                add_up(step - 3, weave.get(step, []))
             if step - 4 in REDUCED:
                 add_up(step - 4)
             for fn, args in tensor_side.get(step, []):

from contextlib import ExitStack

import concourse.mybir as mybir
from concourse.masks import make_identity

B, D, K, N = 1024, 1024, 32, 16
M = K * N
FLOPS = 3 * 2 * B * D * M

F32 = mybir.dt.float32
BF16 = mybir.dt.bfloat16
U32 = mybir.dt.uint32
I32 = mybir.dt.int32
U8 = mybir.dt.uint8
FP8X4 = mybir.dt.float8_e4m3fn_x4
ALU = mybir.AluOpType
ACT = mybir.ActivationFunctionType
AXIS_X = mybir.AxisListType.X

P = 128
PACK = 4
GROUPS = 2
UNITS = 4
QUANTS = N // UNITS
LANES = 32
QUARTER = 128
HALF = 256
GAMMA = 0.97
E_SCALE = B ** -0.5 / N / 2

PHASES = [(0, 0, 2, 0), (0, 2, 2, 0), (1, 0, 2, 0), (1, 2, 2, 0),
          (0, 0, 4, 256), (1, 0, 4, 256), (0, 0, 4, 384), (1, 0, 4, 384)]


REDUCED = (6, 14, 22, 30)


def tile_ensemblequantilehuberheadweightgrad_x2_kernel(
    tc, h, hn, w_words, w_scales, wt_words, wt_scales, r, a, c, out_0, out_1, out_2
):
    nc = tc.nc
    with ExitStack() as ctx:
        keep = ctx.enter_context(tc.tile_pool(name="keep", bufs=1))
        work = ctx.enter_context(tc.tile_pool(name="work", bufs=2))
        psum = ctx.enter_context(tc.psum_pool(name="psum", bufs=2))
        ctx.enter_context(tc.manual_schedule())

        feats = {"h": h, "hn": hn}
        words_in = {"h": w_words, "hn": wt_words}
        scales_in = {"h": w_scales, "hn": wt_scales}
        rows, w_codes, w_planes, w_stage = {}, {}, {}, {}

        def load_rows(op, g, pair):
            t = keep.tile([P, 2, D], BF16, name="rows_%s_%d_%d" % (op, g, pair), align_bytes=256)
            view = feats[op].rearrange("(g p t) f -> g p t f", g=GROUPS, t=PACK)
            nc.sync.dma_start(out=t[:], in_=view[g][:, 2 * pair : 2 * pair + 2, :])
            rows[op, g, pair] = t

        def load_weight(op, half):
            t = keep.tile([P, GROUPS, HALF], U32, name="w_%s_%d" % (op, half), align_bytes=256)
            view = words_in[op].rearrange("g p n t -> p g (n t)")
            nc.sync.dma_start(
                out=t[:].bitcast(I32),
                in_=view[:, :, half * HALF * PACK : (half + 1) * HALF * PACK].bitcast(I32),
            )
            w_codes[op, half] = t

        def load_weight_scales(op):
            t = keep.tile([PACK, GROUPS * 4, M // 4], I32, name="wstage_%s" % op, align_bytes=64)
            view = scales_in[op].rearrange("g (q r) n -> r (g q) n", r=4)
            nc.scalar.dma_start(out=t[:], in_=view.bitcast(I32))
            w_stage[op] = t

        def load_vector(name, vec, queue):
            t = keep.tile([P, GROUPS, PACK], BF16, name=name, align_bytes=64)
            queue.dma_start(out=t[:], in_=vec.rearrange("(g p t) -> p g t", g=GROUPS, t=PACK))
            return t

        def spread_weight_scales(op):
            plane = keep.tile([P, GROUPS, M], U8, name="wplane_%s" % op, align_bytes=64)
            stage = w_stage[op][:].rearrange("r (g q) n -> r q g n", q=4)
            for q in range(4):
                nc.vector.tensor_copy(out=plane[32 * q : 32 * q + 4, :, :].bitcast(I32), in_=stage[:, q])
            w_planes[op] = plane

        load_rows("h", 0, 0)
        load_weight_scales("h")
        load_rows("hn", 0, 0)
        load_weight_scales("hn")
        c_sb = load_vector("c_sb", c, nc.scalar)
        load_weight("h", 0)
        load_weight("hn", 0)
        a_bf = load_vector("a_bf", a, nc.sync)
        r_sb = load_vector("r_sb", r, nc.sync)
        load_rows("h", 0, 1)
        load_rows("hn", 0, 1)
        for pair in range(2):
            load_rows("h", 1, pair)
            load_rows("hn", 1, pair)
        load_weight("h", 1)
        load_weight("hn", 1)

        ident = keep.tile([P, P], F32, name="ident", align_bytes=64)
        make_identity(nc, ident[:])

        factor = keep.tile([P, GROUPS, N, PACK], F32, name="factor", align_bytes=64)
        for low, sign in ((0, 1.0), (N // 2, -1.0)):
            nc.scalar.activation(
                out=factor[:, :, low : low + N // 2, :],
                in_=c_sb[:].unsqueeze(2).broadcast_to([P, GROUPS, N // 2, PACK]),
                func=ACT.Copy,
                scale=sign * E_SCALE,
            )

        a_sb = keep.tile([P, GROUPS, PACK], F32, name="a_sb", align_bytes=64)

        turned, staged, f_codes, f_planes = {}, {}, {}, {}

        def turn(op, g, pair, tag):
            for s in range(2):
                bank = psum.tile([P, GROUPS, 2, P], F32, name="turn", tag=tag)
                words = rows[op, g, pair][:, s, :].bitcast(F32)
                for kg in range(GROUPS):
                    for u in range(2):
                        nc.tensor.transpose(bank[:, kg, u, :], words[:, 256 * kg + u : 256 * (kg + 1) : 2], ident[:])
                turned[op, g, pair, s] = bank

        def unturn(op, g, pair, movers):
            t = work.tile([P, 2, GROUPS, P, 2], F32, name="staged", align_bytes=64)
            for s in range(2):
                movers[s](out=t[:, s], in_=turned[op, g, pair, s][:].rearrange("p kg u b -> p kg b u"))
            staged[op, g, pair] = t

        def quantize_turned(op, g, pair):
            codes = keep.tile([P, 2, GROUPS, P], U32, name="fc_%s_%d_%d" % (op, g, pair), align_bytes=64)
            plane = keep.tile([P, 2, GROUPS, P], U8, name="fp_%s_%d_%d" % (op, g, pair), align_bytes=64)
            nc.vector.quantize_mx(
                out=codes[:].rearrange("p s g b -> p (s g b)").bitcast(FP8X4),
                scales=plane[:].rearrange("p s g b -> p (s g b)"),
                in_=staged[op, g, pair][:].rearrange("p s g b u -> p (s g b u)").bitcast(BF16),
            )
            f_codes[op, g, pair], f_planes[op, g, pair] = codes, plane

        heads, targets, target_rows = {}, {}, {}

        def head_matmuls(op, ph, part):
            g, first, slots, col0 = PHASES[ph]
            width = M // slots
            half, low = divmod(col0, HALF)
            if part == 0:
                heads[op, ph] = psum.tile([P, slots, width], F32, name="head_" + op, bufs=2 if op == "h" else 1)
            for s in range(part * slots // 2, (part + 1) * slots // 2):
                pair, sl = divmod(first + s, 2)
                for kg in range(GROUPS):
                    nc.tensor.matmul_mx(
                        out=heads[op, ph][:, s, :],
                        lhsT=f_codes[op, g, pair][:, sl, kg, :].bitcast(FP8X4),
                        lhsT_scale=f_planes[op, g, pair][:, sl, kg, :],
                        rhs=w_codes[op, half][:, kg, low : low + width].bitcast(FP8X4),
                        rhs_scale=w_planes[op][:, kg, col0 : col0 + width],
                        start=(kg == 0),
                        stop=(kg == GROUPS - 1),
                    )

        def make_targets(ph):
            g, first, slots, col0 = PHASES[ph]
            y = work.tile([P, N, slots, LANES // slots], F32, name="y", align_bytes=64)
            for s in range(slots):
                nc.scalar.activation(
                    out=y[:, :, s, :],
                    in_=heads["hn", ph][:, s, :].rearrange("p (k j) -> p j k", j=N),
                    func=ACT.Identity,
                    scale=GAMMA,
                    bias=r_sb[:, g, first + s : first + s + 1],
                )
            targets[ph] = y
            if any(n // UNITS == ph for n in REDUCED):
                y = work.tile([P, slots, LANES // slots * N], F32, name="y_rows", bufs=1, align_bytes=64)
                for s in range(slots):
                    nc.scalar.activation(
                        out=y[:, s, :], in_=heads["hn", ph][:, s, :], func=ACT.Identity,
                        scale=GAMMA, bias=r_sb[:, g, first + s : first + s + 1],
                    )
                target_rows[ph] = y

        clipped, folded, sums, sums_sb, backs = {}, {}, {}, {}, {}

        def differences(n):
            ph, u = divmod(n, UNITS)
            theta = heads["h", ph][:].rearrange("p s w -> p (s w)").rearrange("p (l i) -> p i l", i=N)[:, QUANTS * u : QUANTS * (u + 1), :]
            if n in REDUCED:
                shape = [P, QUANTS, LANES, N]
                theta = theta.unsqueeze(3).broadcast_to(shape)
                y = target_rows[ph][:].rearrange("p s w -> p (s w)").rearrange("p (l j) -> p l j", j=N)
                y = y.unsqueeze(1).broadcast_to(shape)
            else:
                shape = [P, N, QUANTS, LANES]
                theta = theta.unsqueeze(1).broadcast_to(shape)
                y = targets[ph][:].rearrange("p j s k -> p j (s k)").unsqueeze(2).broadcast_to(shape)
            d = work.tile(shape, F32, name="d", align_bytes=64)
            if u < UNITS // 2:
                nc.vector.tensor_tensor(out=d[:], in0=theta, in1=y, op=ALU.subtract)
            else:
                nc.vector.tensor_tensor(out=d[:], in0=y, in1=theta, op=ALU.subtract)
            return d

        def clip(n, d):
            t = work.tile(list(d.shape), F32, name="clipped", bufs=4, align_bytes=64)
            nc.gpsimd.tensor_scalar(
                out=t[:].rearrange("p x y z -> p (x y z)"),
                in0=d[:].rearrange("p x y z -> p (x y z)"),
                scalar1=1.0, scalar2=-1.0, op0=ALU.min, op1=ALU.max,
            )
            clipped[n] = t

        reduced = {}

        def reduce_over_j(n, absolute):
            t = work.tile([P, 1, QUANTS, LANES], F32, name="reduced", align_bytes=64)
            out = t[:].rearrange("p o i l -> p (o i l)")
            terms = clipped[n][:].rearrange("p i l j -> p (i l) j")
            if absolute:
                nc.vector.tensor_reduce(out=out, in_=terms, axis=AXIS_X, op=ALU.add, apply_absolute_value=True)
            else:
                nc.vector.tensor_reduce(out=out, in_=terms, axis=AXIS_X, op=ALU.add)
            reduced[n, absolute] = t

        def fold(n):
            u = n % UNITS
            if n in REDUCED:
                src = reduced[n, True]
                t = work.tile([P, 1, QUANTS, LANES], F32, name="folded_sum", bufs=1, align_bytes=64)
            else:
                src = clipped[n]
                t = work.tile([P, N, QUANTS, LANES], F32, name="folded", bufs=3, align_bytes=64)
            for i in range(QUANTS):
                slope = abs(2 * (QUANTS * u + i) + 1 - N) / N
                nc.scalar.activation(out=t[:, :, i, :], in_=src[:, :, i, :], func=ACT.Abs, scale=slope)
            folded[n] = t

        def add_up(n, woven=()):
            ph, u = divmod(n, UNITS)
            if u == 0:
                sums[ph] = psum.tile([P, UNITS, P], F32, name="sums", tag="sums")
            plain = reduced[n, False] if n in REDUCED else clipped[n]
            terms = plain.shape[1]
            slots = {0: (), 1: (3,), 2: (1, 3)}[len(woven)]
            for j in range(terms):
                slot = j // 4 if j % 4 == 3 else None
                for second, src in enumerate((plain, folded[n])):
                    as_product = second == 1 and slot is not None and slot not in slots
                    nc.tensor.matmul(
                        out=sums[ph][:, u, :],
                        lhsT=src[:, j].rearrange("p i l -> p (i l)"),
                        rhs=ident[:],
                        is_transpose=not as_product,
                        start=(j == 0 and second == 0),
                        stop=(j == terms - 1 and second == 1),
                    )
                if slot in slots:
                    fn, args = woven[slots.index(slot)]
                    fn(*args)

        def sums_out(ph):
            t = work.tile([P, UNITS, P], F32, name="sums_sb", align_bytes=64)
            nc.scalar.copy(out=t[:], in_=sums[ph][:])
            sums_sb[ph] = t

        def turn_back(ph):
            bank = psum.tile([P, UNITS, P], F32, name="back", bufs=1)
            for u in range(UNITS):
                nc.tensor.transpose(bank[:, u, :], sums_sb[ph][:, u, :], ident[:])
            backs[ph] = bank

        e_bf, e_codes, e_planes = {}, {}, {}

        def weigh(ph):
            g, first, slots, col0 = PHASES[ph]
            members = LANES // slots
            if first == 0:
                e_bf[g, col0] = keep.tile([P, members, N, PACK], BF16, name="e_%d_%d" % (g, col0), align_bytes=64)
            nc.vector.tensor_tensor(
                out=e_bf[g, col0][:, :, :, first : first + slots],
                in0=backs[ph][:].rearrange("p u l -> p (u l)").rearrange("p (i s k) -> p k i s", i=N, s=slots),
                in1=factor[:, g, :, first : first + slots].unsqueeze(1).broadcast_to([P, members, N, slots]),
                op=ALU.mult,
            )

        def quantize_e(ph):
            g, first, slots, col0 = PHASES[ph]
            width = M // slots
            codes = keep.tile([P, width], U32, name="ec_%d_%d" % (g, col0), align_bytes=64)
            plane = keep.tile([P, width], U8, name="ep_%d_%d" % (g, col0), align_bytes=64)
            nc.vector.quantize_mx(
                out=codes[:].bitcast(FP8X4),
                scales=plane[:],
                in_=e_bf[g, col0][:].rearrange("p k i t -> p (k i t)"),
            )
            for low in range(0, width, QUARTER):
                e_codes[g, (col0 + low) // QUARTER] = codes[:, low : low + QUARTER]
                e_planes[g, (col0 + low) // QUARTER] = plane[:, low : low + QUARTER]

        scaled, laid, ha_codes, ha_planes = {}, {}, {}, {}

        def scale_rows(g, t):
            if t == 0:
                scaled[g] = work.tile([P, PACK, D], BF16, name="scaled", align_bytes=64)
            src = rows["h", g, t // 2][:, t % 2, :]
            if g == 0:
                nc.vector.tensor_scalar(
                    out=scaled[g][:, t, :], in0=src, scalar1=a_sb[:, g, t : t + 1], scalar2=None, op0=ALU.mult
                )
            else:
                nc.scalar.activation(out=scaled[g][:, t, :], in_=src, func=ACT.Copy, scale=a_sb[:, g, t : t + 1])

        def lay_rows(g, fg):
            t = work.tile([P, PACK, P, PACK], BF16, name="laid", align_bytes=64)
            nc.gpsimd.tensor_scalar(
                out=t[:],
                in0=scaled[g][:, :, 512 * fg : 512 * (fg + 1)].rearrange("p t (m v) -> p v m t", v=PACK),
                scalar1=1.0, scalar2=0.0, op0=ALU.mult, op1=ALU.add,
            )
            laid[g, fg] = t

        def quantize_laid(g, fg):
            codes = keep.tile([P, PACK, P], U32, name="hc_%d_%d" % (g, fg), align_bytes=64)
            plane = keep.tile([P, PACK, P], U8, name="hp_%d_%d" % (g, fg), align_bytes=64)
            nc.vector.quantize_mx(
                out=codes[:].rearrange("p v m -> p (v m)").bitcast(FP8X4),
                scales=plane[:].rearrange("p v m -> p (v m)"),
                in_=laid[g, fg][:].rearrange("p v m t -> p (v m t)"),
            )
            ha_codes[g, fg], ha_planes[g, fg] = codes, plane

        grads, grads_bf = {}, {}

        def grad_matmuls(q, part):
            fg, low = divmod(2 * part, PACK)
            if low == 0:
                grads[q, fg] = psum.tile([P, PACK, QUARTER], F32, name="grad", tag="aux")
            for v in range(low, low + 2):
                for g in range(GROUPS):
                    nc.tensor.matmul_mx(
                        out=grads[q, fg][:, v, :],
                        lhsT=ha_codes[g, fg][:, v, :].bitcast(FP8X4),
                        lhsT_scale=ha_planes[g, fg][:, v, :],
                        rhs=e_codes[g, q].bitcast(FP8X4),
                        rhs_scale=e_planes[g, q],
                        start=(g == 0),
                        stop=(g == GROUPS - 1),
                    )

        def store_grad(q, fg):
            t = work.tile([P, PACK, QUARTER], F32, name="grad_sb", bufs=4, align_bytes=64)
            nc.scalar.copy(out=t[:], in_=grads[q, fg][:])
            view = out_0.rearrange("(g p v) m -> g p v m", g=GROUPS, v=PACK)
            nc.sync.dma_start(out=view[fg][:, :, q * QUARTER : (q + 1) * QUARTER], in_=t[:])

        def round_grad(q, fg, mover):
            if q not in grads_bf:
                grads_bf[q] = work.tile([P, GROUPS, QUARTER, PACK], BF16, name="grad_bf", align_bytes=64)
            mover(out=grads_bf[q][:, fg], in_=grads[q, fg][:].rearrange("p v m -> p m v"))

        def store_planes(q):
            codes = work.tile([P, GROUPS, QUARTER], U32, name="out_codes", align_bytes=64)
            plane = work.tile([P, GROUPS, QUARTER], U8, name="out_plane", align_bytes=64)
            nc.vector.quantize_mx(
                out=codes[:].rearrange("p g m -> p (g m)").bitcast(FP8X4),
                scales=plane[:].rearrange("p g m -> p (g m)"),
                in_=grads_bf[q][:].rearrange("p g m v -> p (g m v)"),
            )
            word_view = out_1.rearrange("g p m t -> p g (m t)")
            nc.sync.dma_start(
                out=word_view[:, :, q * QUARTER * PACK : (q + 1) * QUARTER * PACK].bitcast(I32),
                in_=codes[:].bitcast(I32),
            )
            scale_view = out_2.rearrange("g s m -> s g m")
            for quad in range(4):
                nc.sync.dma_start(
                    out=scale_view[4 * quad : 4 * quad + 4, :, q * QUARTER : (q + 1) * QUARTER].bitcast(I32),
                    in_=plane[32 * quad : 32 * quad + 4, :, :].bitcast(I32),
                )

        both = (nc.scalar.copy, nc.vector.tensor_copy)
        scalar_only = (nc.scalar.copy, nc.scalar.copy)

        turn("h", 0, 0, "aux")
        turn("hn", 0, 0, "sums")
        spread_weight_scales("h")
        spread_weight_scales("hn")
        nc.vector.tensor_copy(out=a_sb[:], in_=a_bf[:])
        unturn("h", 0, 0, both)
        scale_rows(0, 0)
        quantize_turned("h", 0, 0)
        unturn("hn", 0, 0, both)
        scale_rows(0, 1)
        quantize_turned("hn", 0, 0)
        for op in ("h", "hn"):
            for part in range(2):
                head_matmuls(op, 0, part)
        make_targets(0)
        turn("h", 0, 1, "aux")
        scale_rows(0, 2)
        scale_rows(0, 3)
        lay_rows(0, 0)

        port, vector_side, pool_side, scalar_side, tensor_side, weave = {}, {}, {}, {}, {}, {}

        def at(table, step, fn, *args):
            table.setdefault(step, []).append((fn, args))

        for op, g, pair, turn_at, quantize_at in (
            ("h", 0, 1, -1, 1), ("hn", 0, 1, 0, 2), ("h", 1, 0, 1, 3), ("hn", 1, 0, 2, 4),
            ("h", 1, 1, 4, 6), ("hn", 1, 1, 6, 9),
        ):
            at(tensor_side, turn_at, turn, op, g, pair, "aux")
            at(scalar_side, turn_at + 1, unturn, op, g, pair, scalar_only)
            at(port, quantize_at, quantize_turned, op, g, pair)
        for ph in range(len(PHASES)):
            if ph > 0:
                steps = (1, 1, 2, 2) if ph == 1 else range(4 * ph - 5, 4 * ph - 1)
                for step, (op, part) in zip(steps, (("h", 0), ("h", 1), ("hn", 0), ("hn", 1))):
                    if ph == 1:
                        at(tensor_side, step, head_matmuls, op, ph, part)
                    else:
                        at(weave, step + 1 if step - 3 in REDUCED else step, head_matmuls, op, ph, part)
                at(scalar_side, 4 * ph - 1, make_targets, ph)
            at(scalar_side, 4 * ph + 7, sums_out, ph)
            at(tensor_side, 4 * ph + 7, turn_back, ph)
            at(vector_side, 4 * ph + 8, weigh, ph)
            if PHASES[ph][1] + PHASES[ph][2] == PACK:
                at(port, 4 * ph + 9, quantize_e, ph)
        for n in REDUCED:
            at(vector_side, n + 1, reduce_over_j, n, False)
            at(vector_side, n + 2, reduce_over_j, n, True)
            at(scalar_side, n + 3, fold, n)
        for t, step in enumerate((8, 8, 11, 12)):
            at(scalar_side, step, scale_rows, 1, t)
        for step, g, fg in ((7, 0, 1), (15, 1, 0), (16, 1, 1)):
            at(pool_side, step, lay_rows, g, fg)
        for step, g, fg in ((5, 0, 0), (10, 0, 1), (18, 1, 0), (19, 1, 1)):
            at(port, step, quantize_laid, g, fg)
        for q, steps, planes_at in ((0, (22, 23, 24, 27), 30), (1, (27, 28, 29, 29), 31), (2, (30, 31, 32, 32), 34)):
            for part in range(4):
                at(weave, steps[part], grad_matmuls, q, part)
            for fg in range(GROUPS):
                at(scalar_side, steps[2 * fg + 1] + 1, store_grad, q, fg)
                at(scalar_side, steps[2 * fg + 1] + 1, round_grad, q, fg, nc.scalar.copy)
            at(port, planes_at, store_planes, q)

        units = UNITS * len(PHASES)
        for step in range(units + 6):
            if step < units:
                d = differences(step)
            for fn, args in port.get(step, []):
                fn(*args)
            if step < units:
                clip(step, d)
            if 2 <= step < units + 2 and step - 2 not in REDUCED:
                fold(step - 2)
            for table in (vector_side, pool_side, scalar_side):
                for fn, args in table.get(step, []):
                    fn(*args)
            if 3 <= step < units + 3 and step - 3 not in REDUCED:
                add_up(step - 3, weave.get(step, []))
            if step - 4 in REDUCED:
                add_up(step - 4)
            for fn, args in tensor_side.get(step, []):
                fn(*args)

        last = 3
        for part in range(4):
            grad_matmuls(last, part)
        store_grad(last, 0)
        round_grad(last, 1, nc.vector.tensor_copy)
        store_grad(last, 1)
        round_grad(last, 0, nc.vector.tensor_copy)
        store_planes(last)
